import numpy as np
import ml_dtypes


def mxq(x, axis, fmt="e4m3"):
    dtype, down = {"e4m3": (ml_dtypes.float8_e4m3fn, 7), "e5m2": (ml_dtypes.float8_e5m2, 14)}[fmt]
    v = np.moveaxis(np.asarray(x, np.float32).astype(ml_dtypes.bfloat16).astype(np.float64), axis, -1)
    blocks = v.reshape(v.shape[:-1] + (-1, 32))
    amax = np.abs(blocks).max(-1, keepdims=True)
    byte = np.maximum(np.where(amax > 0, np.frexp(amax)[1] - 1 + 127, 0) - down, 1)
    scale = np.exp2(byte - 127.0)
    codes = (blocks / scale).astype(np.float32).astype(dtype).astype(np.float64)
    return np.moveaxis((codes * scale).reshape(v.shape), -1, axis)


WIDE = False


def mx_kscale(k):
    if not WIDE:
        return np.ones(k)
    levels = np.array([10, -10, 5, -5, 0])
    if k % 512:
        return np.exp2(np.random.permutation(np.resize(levels, k // 32))).repeat(32)
    a = np.empty((k // 512, 16))
    for p in range(k // 512):
        a[p, :8] = np.random.permutation(np.resize(levels, 8))
        for g in range(8):
            far = levels[np.abs(levels - a[p, g]) >= 10]
            a[p, g + 8] = far[np.random.randint(len(far))]
    return np.exp2(a.ravel()).repeat(32)


def f64(x):
    return np.asarray(x).astype(np.float64)


def striped(idx):
    return np.tile(idx.reshape(-1, 16).T, (8, 1)).astype(np.uint16)


def unstriped(offs):
    return offs[:16].T.reshape(-1).astype(np.int64)


E2M1 = np.array([0.0, 0.5, 1.0, 1.5, 2.0, 3.0, 4.0, 6.0, -0.0, -0.5, -1.0, -1.5, -2.0, -3.0, -4.0, -6.0])


def pack_weight(w, fmt):
    k, n = w.shape
    w = f64(np.asarray(w, np.float32).astype(ml_dtypes.bfloat16)).reshape(k // 32, 32, n)
    amax = np.abs(w).max(1)
    if fmt == "e4m3":
        byte = np.frexp(amax)[1] - 1 + 127 - 7
    else:
        mant, ex = np.frexp(amax / 6.0)
        byte = np.where(mant > 0.5, ex, ex - 1) + 127
    byte = np.clip(np.where(amax > 0, byte, 1), 1, 254)
    scaled = (w * np.exp2(127.0 - byte)[:, None, :]).reshape(k, n).astype(np.float32)
    by_word = np.ascontiguousarray(scaled.reshape(k // 512, 128, 4, n).transpose(0, 1, 3, 2))
    if fmt == "e4m3":
        words = by_word.astype(ml_dtypes.float8_e4m3fn).view(np.uint8)
    else:
        c = by_word.astype(ml_dtypes.float4_e2m1fn).view(np.uint8) & 0xF
        words = (c[..., 0::2] | (c[..., 1::2] << 4)).reshape(k // 512, 128, 2 * n)
    return np.ascontiguousarray(words), np.ascontiguousarray(byte.astype(np.uint8).reshape(k // 512, 16, n))


def unpack_weight(words, scales, fmt):
    g, _, n = scales.shape
    words = np.ascontiguousarray(words).reshape(g, 128, n, -1)
    if fmt == "e4m3":
        vals = words.view(ml_dtypes.float8_e4m3fn).astype(np.float64)
    else:
        nib = np.empty((g, 128, n, 4), np.uint8)
        nib[..., 0::2] = words & 0xF
        nib[..., 1::2] = words >> 4
        vals = E2M1[nib]
    vals = vals * np.repeat(np.exp2(scales.astype(np.float64) - 127.0), 8, axis=1)[..., None]
    return vals.transpose(0, 1, 3, 2).reshape(g * 512, n)


def gelu(v):
    return 0.5 * v * (1.0 + np.tanh(np.sqrt(2.0 / np.pi) * (v + 0.044715 * v**3)))


K, T, S, H, T2, P, N = 1536, 2048, 1024, 512, 2048, 1024, 768


def setup_inputs():
    n = np.random.standard_normal
    s = mx_kscale(K)[:, None]
    u = mx_kscale(H)[:, None]
    tab_words, tab_scales = pack_weight(n((K, T)) * s, "e4m3")
    wc_words, wc_scales = pack_weight(n((K, H)) * 0.9 / np.sqrt(K) / s * u.T, "e2m1")
    wf = (n((K, H)) * 0.5 / np.sqrt(K) / s * u.T).astype(np.float32)
    gain = np.exp(0.3 * n(H)).astype(np.float32)
    page0 = (n((H, T2)) * u).astype(np.float32)
    w2 = (n((H, N)) * 1.3 / np.sqrt(H) / u).astype(np.float32)
    rel = np.exp(0.4 * n((N, P))).astype(np.float32)
    offs = striped(np.random.permutation(T)[:S])
    offs2 = striped(np.random.permutation(T2)[:S])
    offs3 = striped(np.random.permutation(T2)[:P])
    return {"tab_words": tab_words, "tab_scales": tab_scales, "offs": offs,
            "wc_words": wc_words, "wc_scales": wc_scales, "wf": wf, "gain": gain,
            "page0": page0, "offs2": offs2, "offs3": offs3, "w2": w2, "rel": rel}


def reference(tab_words, tab_scales, offs, wc_words, wc_scales, wf, gain,
              page0, offs2, offs3, w2, rel):
    v = unpack_weight(tab_words, tab_scales, "e4m3")[:, unstriped(offs)]
    wc = unpack_weight(wc_words, wc_scales, "e2m1")
    h = f64(gain)[:, None] * (wc.T @ v + mxq(f64(wf), 0, "e4m3").T @ v)
    page = f64(page0).copy()
    l2 = unstriped(offs2)
    page[:, l2] = np.maximum(page[:, l2], h)
    x = page[:, unstriped(offs3)]
    y = mxq(f64(w2), 0, "e4m3").T @ mxq(x, 0, "e4m3")
    return f64(rel) * np.tanh(y)

@@ -1,0 +1,226 @@
+from contextlib import ExitStack
+
+import concourse.mybir as mybir
+
+K, T, S, H, T2, M, N = 1536, 2048, 1024, 512, 2048, 1024, 768
+FLOPS = 2 * (2 * K * H * S + H * N * M)
+
+F32 = mybir.dt.float32
+BF16 = mybir.dt.bfloat16
+I32 = mybir.dt.int32
+U32 = mybir.dt.uint32
+U16 = mybir.dt.uint16
+U8 = mybir.dt.uint8
+FP8X4 = mybir.dt.float8_e4m3fn_x4
+FP4X4 = mybir.dt.float4_e2m1fn_x4
+ALU = mybir.AluOpType
+ACT = mybir.ActivationFunctionType
+
+P = 128
+PACK = 4
+PASSES = K // (P * PACK)
+QUADS = 4
+RUN = 8
+BANK = 512
+HALVES = S // BANK
+CHUNK = 256
+CHUNKS = M // CHUNK
+N_TILES = N // P
+PER_BANK = BANK // CHUNK
+LIST_COL = 16
+SCALE_ROW0 = 20
+MOVED_ROWS = 100
+H_BANKS = 3
+
+
+def tile_list_lost_property_profiles_kernel(
+    tc, tab_words, tab_scales, offs, wc_words, wc_scales, wf, gain, page0, offs2, offs3, w2, rel, out
+):
+    nc = tc.nc
+    with ExitStack() as ctx:
+        keep = ctx.enter_context(tc.tile_pool(name="keep", bufs=1))
+        psum = ctx.enter_context(tc.psum_pool(name="psum", bufs=1))
+
+        def sb(name, shape, dtype, tag=None):
+            return keep.tile(shape, dtype, name=name, tag=tag or name, align_bytes=64)
+
+        idx = sb("idx", [P, S // LIST_COL], U16)
+        idx2 = sb("idx2", [P, S // LIST_COL], U16)
+        idx3 = sb("idx3", [P, M // LIST_COL], U16)
+        tab = [sb("tab%d" % a, [P, T], U32) for a in range(PASSES)]
+        tab_sc = sb("tab_sc", [P, T], U8)
+        v_planes = sb("v_planes", [P, PASSES * S], U8)
+        wc_raw = sb("wc_raw", [P, PASSES * 2 * H], U8)
+        wc_sc_raw = sb("wc_sc_raw", [P, PASSES * H], U8)
+        wf_raw = [sb("wf_raw%d" % a, [P, PACK, H], F32) for a in range(PASSES)]
+        page = [sb("page%d" % t, [P, T2], F32) for t in range(PACK)]
+        gains = [sb("gain%d" % t, [P, 1], F32) for t in range(PACK)]
+        w2_raw = sb("w2_raw", [P, PACK, N], F32)
+        rel_sb = sb("rel_sb", [P, N_TILES, M], F32)
+
+        for q in range(QUADS):
+            nc.vector.memset(tab_sc[32 * q : 32 * q + SCALE_ROW0, :].bitcast(I32), 0)
+        nc.gpsimd.memset(wc_sc_raw[:].bitcast(I32), 0)
+        nc.gpsimd.memset(v_planes[:].bitcast(I32), 0)
+
+        def load_tab(a, queue):
+            words = tab_words[a].rearrange("p t i -> p (t i)").bitcast(I32)
+            queue.dma_start(out=tab[a][:].bitcast(I32), in_=words)
+
+        def load_wf(a):
+            rows = wf[a * P * PACK : (a + 1) * P * PACK, :]
+            nc.sync.dma_start(out=wf_raw[a][:], in_=rows.rearrange("(p j) c -> p j c", j=PACK))
+
+        page_rows = page0.rearrange("(g t q) c -> t g q c", t=PACK, q=RUN)
+        w2_rows = w2.rearrange("(g t q) c -> t g q c", t=PACK, q=RUN)
+        gain_rows = gain.rearrange("(g t q o) -> t g q o", t=PACK, q=RUN, o=1)
+
+        nc.sync.dma_start(idx[:], offs)
+        load_tab(0, nc.scalar)
+        for q in range(QUADS):
+            (nc.sync, nc.scalar)[q % 2].dma_start(
+                out=tab_sc[32 * q + SCALE_ROW0 : 32 * (q + 1), :].bitcast(I32),
+                in_=tab_scales[:, 4 * q : 4 * q + 4, :].bitcast(I32),
+            )
+        load_tab(1, nc.sync)
+        load_tab(2, nc.sync)
+        nc.sync.dma_start(
+            out=wc_raw[:].bitcast(I32).rearrange("p (a w) -> p a w", a=PASSES),
+            in_=wc_words.bitcast(I32).rearrange("a p w -> p a w"),
+        )
+        for q in range(QUADS):
+            nc.sync.dma_start(
+                out=wc_sc_raw[32 * q : 32 * q + 4, :].bitcast(I32).rearrange("r (a w) -> r a w", a=PASSES),
+                in_=wc_scales[:, 4 * q : 4 * q + 4, :].bitcast(I32).rearrange("a r w -> r a w"),
+            )
+        load_wf(0)
+        load_wf(1)
+        load_wf(2)
+        nc.sync.dma_start(idx2[:], offs2)
+        nc.sync.dma_start(out=page[0][:], in_=page_rows[0])
+        with nc.allow_non_contiguous_dma(reason="one gain value for each partition"):
+            for t in range(PACK):
+                nc.sync.dma_start(out=gains[t][:], in_=gain_rows[t])
+        for t in range(1, PACK):
+            nc.sync.dma_start(out=page[t][:], in_=page_rows[t])
+        for t in range(PACK):
+            nc.sync.dma_start(out=w2_raw[:, t, :], in_=w2_rows[t])
+        nc.sync.dma_start(idx3[:], offs3)
+        nc.sync.dma_start(out=rel_sb[:], in_=rel.rearrange("(j p) m -> p j m", p=P))
+
+        v_words = [sb("v_words%d" % a, [P, S], U32) for a in range(PASSES)]
+        v_sc = sb("v_sc", [P, S], U8)
+        nc.vector.tensor_copy(v_sc[:], tab_sc[:].indirect(idx[:]))
+        for a in range(PASSES):
+            nc.vector.tensor_copy(v_words[a][:], tab[a][:].indirect(idx[:]))
+        for a in range(PASSES):
+            row0 = SCALE_ROW0 + 4 * a
+            nc.scalar.dma_start(
+                out=v_planes[0:MOVED_ROWS, a * S : (a + 1) * S].bitcast(I32),
+                in_=v_sc[row0 : row0 + MOVED_ROWS, :].bitcast(I32),
+            )
+
+        wc_codes = sb("wc_codes", [P, PASSES * 2 * H], U8)
+        wc_planes = sb("wc_planes", [P, PASSES * H], U8)
+        for dealt, raw, words in ((wc_codes, wc_raw, RUN // 2), (wc_planes, wc_sc_raw, RUN // 4)):
+            nc.vector.tensor_copy(
+                out=dealt[:].bitcast(I32).rearrange("p (a t g w) -> p a t g w", a=PASSES, t=PACK, w=words),
+                in_=raw[:].bitcast(I32).rearrange("p (a g t w) -> p a t g w", a=PASSES, t=PACK, w=words),
+            )
+
+        wf_codes = [sb("wf_codes%d" % a, [P, H], U32) for a in range(PASSES)]
+        wf_planes = [sb("wf_planes%d" % a, [P, H], U8) for a in range(PASSES)]
+        for a in range(PASSES):
+            src = wf_raw[a][:].rearrange("p j (g t q) -> p t g q j", t=PACK, q=RUN)
+            for t in range(PACK):
+                woven = sb("wf_woven%d_%d" % (a, t), [P, P * PACK], BF16)
+                nc.scalar.copy(out=woven[:].rearrange("p (g q j) -> p g q j", q=RUN, j=PACK), in_=src[:, t])
+                cols = slice(t * P, (t + 1) * P)
+                nc.vector.quantize_mx(
+                    out=wf_codes[a][:, cols].bitcast(FP8X4), scales=wf_planes[a][:, cols], in_=woven[:]
+                )
+
+        for t in range(PACK):
+            fresh = sb("fresh%d" % t, [P, S], F32)
+            banks = []
+            for u in range(HALVES):
+                bank = psum.tile([P, BANK], F32, name="h%d_%d" % (t, u), tag="bank%d" % ((HALVES * t + u) % H_BANKS))
+                banks.append(bank)
+                cols = slice(u * BANK, (u + 1) * BANK)
+                for a in range(PASSES):
+                    c0 = a * H + t * P
+                    nc.tensor.matmul_mx(
+                        out=bank[:],
+                        lhsT=wc_codes[:, 2 * c0 : 2 * (c0 + P)].bitcast(FP4X4),
+                        lhsT_scale=wc_planes[:, c0 : c0 + P],
+                        rhs=v_words[a][:, cols].bitcast(FP8X4),
+                        rhs_scale=v_planes[:, a * S + u * BANK : a * S + (u + 1) * BANK],
+                        start=(a == 0),
+                        stop=False,
+                    )
+                for a in range(PASSES):
+                    nc.tensor.matmul_mx(
+                        out=bank[:],
+                        lhsT=wf_codes[a][:, t * P : (t + 1) * P].bitcast(FP8X4),
+                        lhsT_scale=wf_planes[a][:, t * P : (t + 1) * P],
+                        rhs=v_words[a][:, cols].bitcast(FP8X4),
+                        rhs_scale=v_planes[:, a * S + u * BANK : a * S + (u + 1) * BANK],
+                        start=False,
+                        stop=(a == PASSES - 1),
+                    )
+            for u in range(HALVES):
+                part = idx2[:, u * BANK // LIST_COL : (u + 1) * BANK // LIST_COL]
+                nc.vector.tensor_copy(fresh[:, u * BANK : (u + 1) * BANK], page[t][:].indirect(part))
+            for u in range(HALVES):
+                cols = slice(u * BANK, (u + 1) * BANK)
+                nc.vector.scalar_tensor_tensor(
+                    out=fresh[:, cols], in0=banks[u][:], scalar=gains[t][:], in1=fresh[:, cols],
+                    op0=ALU.mult, op1=ALU.max,
+                )
+            nc.vector.tensor_copy(page[t][:].indirect(idx2[:]), fresh[:])
+
+        w2_codes = sb("w2_codes", [P, N], U32)
+        w2_plane = sb("w2_plane", [P, N], U8)
+        w2_woven = sb("w2_woven", [P, N, PACK], BF16)
+        for u in range(2):
+            cols = slice(u * N // 2, (u + 1) * N // 2)
+            nc.scalar.copy(out=w2_woven[:, cols, :], in_=w2_raw[:, :, cols].rearrange("p t n -> p n t"))
+            nc.vector.quantize_mx(
+                out=w2_codes[:, cols].bitcast(FP8X4), scales=w2_plane[:, cols],
+                in_=w2_woven[:, cols, :].rearrange("p n t -> p (n t)"),
+            )
+
+        out_rows = out.rearrange("(j p) m -> p j m", p=P)
+        picked_tags = ["picked0", "fresh3", "x_woven0", "x_woven1"]
+        for c in range(CHUNKS):
+            part = idx3[:, c * CHUNK // LIST_COL : (c + 1) * CHUNK // LIST_COL]
+            picked = sb("picked%d" % c, [P, PACK, CHUNK], F32, tag=picked_tags[c])
+            for t in range(PACK):
+                nc.vector.tensor_copy(picked[:, t, :], page[t][:].indirect(part))
+            woven = sb("x_woven%d" % c, [P, CHUNK, PACK], BF16)
+            nc.scalar.copy(out=woven[:], in_=picked[:].rearrange("p t m -> p m t"))
+            x_codes = sb("x_codes%d" % c, [P, CHUNK], U32)
+            x_plane = sb("x_plane%d" % c, [P, CHUNK], U8)
+            nc.vector.quantize_mx(
+                out=x_codes[:].bitcast(FP8X4), scales=x_plane[:], in_=woven[:].rearrange("p m t -> p (m t)")
+            )
+            cols = slice(c * CHUNK, (c + 1) * CHUNK)
+            for b in range(N_TILES // PER_BANK):
+                slot = (c * (N_TILES // PER_BANK) + b) % (PACK * HALVES)
+                bank = psum.tile([P, PER_BANK, CHUNK], F32, name="y%d_%d" % (c, b), tag="bank%d" % slot)
+                for i in range(PER_BANK):
+                    j = PER_BANK * b + i
+                    nc.tensor.matmul_mx(
+                        out=bank[:, i, :],
+                        lhsT=w2_codes[:, j * P : (j + 1) * P].bitcast(FP8X4),
+                        lhsT_scale=w2_plane[:, j * P : (j + 1) * P],
+                        rhs=x_codes[:].bitcast(FP8X4),
+                        rhs_scale=x_plane[:],
+                        start=True,
+                        stop=True,
+                    )
+                res = sb("res%d_%d" % (c, b), [P, PER_BANK, CHUNK], F32)
+                nc.scalar.activation(out=res[:], in_=bank[:], func=ACT.Tanh)
+                rows = slice(PER_BANK * b, PER_BANK * (b + 1))
+                nc.vector.tensor_tensor(out=res[:], in0=res[:], in1=rel_sb[:, rows, cols], op=ALU.mult)
+                nc.sync.dma_start(out=out_rows[:, rows, cols], in_=res[:])

@@ -31,6 +31,7 @@ LIST_COL = 16
 SCALE_ROW0 = 20
 MOVED_ROWS = 100
 H_BANKS = 3
+LINE = 4
 
 
 def tile_list_lost_property_profiles_kernel(
@@ -43,6 +44,11 @@ def tile_list_lost_property_profiles_kernel(
 
         def sb(name, shape, dtype, tag=None):
             return keep.tile(shape, dtype, name=name, tag=tag or name, align_bytes=64)
+
+        def weave(dst, src):
+            nc.scalar.copy(
+                out=dst.rearrange("p (c i) t -> p c t i", i=LINE), in_=src.rearrange("p t (c i) -> p c t i", i=LINE)
+            )
 
         idx = sb("idx", [P, S // LIST_COL], U16)
         idx2 = sb("idx2", [P, S // LIST_COL], U16)
@@ -83,7 +89,6 @@ def tile_list_lost_property_profiles_kernel(
                 in_=tab_scales[:, 4 * q : 4 * q + 4, :].bitcast(I32),
             )
         load_tab(1, nc.sync)
-        load_tab(2, nc.sync)
         nc.sync.dma_start(
             out=wc_raw[:].bitcast(I32).rearrange("p (a w) -> p a w", a=PASSES),
             in_=wc_words.bitcast(I32).rearrange("a p w -> p a w"),
@@ -93,20 +98,22 @@ def tile_list_lost_property_profiles_kernel(
                 out=wc_sc_raw[32 * q : 32 * q + 4, :].bitcast(I32).rearrange("r (a w) -> r a w", a=PASSES),
                 in_=wc_scales[:, 4 * q : 4 * q + 4, :].bitcast(I32).rearrange("a r w -> r a w"),
             )
+        load_tab(2, nc.sync)
         load_wf(0)
-        load_wf(1)
-        load_wf(2)
         nc.sync.dma_start(idx2[:], offs2)
         nc.sync.dma_start(out=page[0][:], in_=page_rows[0])
+        load_wf(1)
+        load_wf(2)
         with nc.allow_non_contiguous_dma(reason="one gain value for each partition"):
             for t in range(PACK):
                 nc.sync.dma_start(out=gains[t][:], in_=gain_rows[t])
-        for t in range(1, PACK):
-            nc.sync.dma_start(out=page[t][:], in_=page_rows[t])
+        nc.sync.dma_start(out=page[1][:], in_=page_rows[1])
+        nc.sync.dma_start(idx3[:], offs3)
         for t in range(PACK):
             nc.sync.dma_start(out=w2_raw[:, t, :], in_=w2_rows[t])
-        nc.sync.dma_start(idx3[:], offs3)
+        nc.sync.dma_start(out=page[2][:], in_=page_rows[2])
         nc.sync.dma_start(out=rel_sb[:], in_=rel.rearrange("(j p) m -> p j m", p=P))
+        nc.sync.dma_start(out=page[3][:], in_=page_rows[3])
 
         v_words = [sb("v_words%d" % a, [P, S], U32) for a in range(PASSES)]
         v_sc = sb("v_sc", [P, S], U8)
@@ -131,13 +138,17 @@ def tile_list_lost_property_profiles_kernel(
         wf_codes = [sb("wf_codes%d" % a, [P, H], U32) for a in range(PASSES)]
         wf_planes = [sb("wf_planes%d" % a, [P, H], U8) for a in range(PASSES)]
         for a in range(PASSES):
-            src = wf_raw[a][:].rearrange("p j (g t q) -> p t g q j", t=PACK, q=RUN)
-            for t in range(PACK):
-                woven = sb("wf_woven%d_%d" % (a, t), [P, P * PACK], BF16)
-                nc.scalar.copy(out=woven[:].rearrange("p (g q j) -> p g q j", q=RUN, j=PACK), in_=src[:, t])
-                cols = slice(t * P, (t + 1) * P)
+            src = wf_raw[a][:].rearrange("p j (g t h i) -> p t g h j i", t=PACK, h=RUN // LINE, i=LINE)
+            step = 1 if a == PASSES - 1 else PACK
+            for t0 in range(0, PACK, step):
+                woven = sb("wf_woven%d_%d" % (a, t0), [P, step, P * PACK], BF16)
+                for t in range(t0, t0 + step):
+                    dst = woven[:, t - t0, :].rearrange("p (g h i j) -> p g h j i", h=RUN // LINE, i=LINE, j=PACK)
+                    nc.scalar.copy(out=dst, in_=src[:, t])
+                cols = slice(t0 * P, (t0 + step) * P)
                 nc.vector.quantize_mx(
-                    out=wf_codes[a][:, cols].bitcast(FP8X4), scales=wf_planes[a][:, cols], in_=woven[:]
+                    out=wf_codes[a][:, cols].bitcast(FP8X4), scales=wf_planes[a][:, cols],
+                    in_=woven[:].rearrange("p t w -> p (t w)"),
                 )
 
         for t in range(PACK):
@@ -184,29 +195,36 @@ def tile_list_lost_property_profiles_kernel(
         w2_woven = sb("w2_woven", [P, N, PACK], BF16)
         for u in range(2):
             cols = slice(u * N // 2, (u + 1) * N // 2)
-            nc.scalar.copy(out=w2_woven[:, cols, :], in_=w2_raw[:, :, cols].rearrange("p t n -> p n t"))
+            weave(w2_woven[:, cols, :], w2_raw[:, :, cols])
             nc.vector.quantize_mx(
                 out=w2_codes[:, cols].bitcast(FP8X4), scales=w2_plane[:, cols],
                 in_=w2_woven[:, cols, :].rearrange("p n t -> p (n t)"),
             )
 
         out_rows = out.rearrange("(j p) m -> p j m", p=P)
-        picked_tags = ["picked0", "fresh3", "x_woven0", "x_woven1"]
-        for c in range(CHUNKS):
+        groups = N_TILES // PER_BANK
+        picked_tags = ["picked0", "fresh3", "x_woven0", "curve0_%d" % (groups - 1)]
+        picked, x_codes, x_planes = {}, {}, {}
+
+        def pick(c):
             part = idx3[:, c * CHUNK // LIST_COL : (c + 1) * CHUNK // LIST_COL]
-            picked = sb("picked%d" % c, [P, PACK, CHUNK], F32, tag=picked_tags[c])
+            picked[c] = sb("picked%d" % c, [P, PACK, CHUNK], F32, tag=picked_tags[c])
             for t in range(PACK):
-                nc.vector.tensor_copy(picked[:, t, :], page[t][:].indirect(part))
+                nc.vector.tensor_copy(picked[c][:, t, :], page[t][:].indirect(part))
+
+        def quantise(c):
             woven = sb("x_woven%d" % c, [P, CHUNK, PACK], BF16)
-            nc.scalar.copy(out=woven[:], in_=picked[:].rearrange("p t m -> p m t"))
-            x_codes = sb("x_codes%d" % c, [P, CHUNK], U32)
-            x_plane = sb("x_plane%d" % c, [P, CHUNK], U8)
+            weave(woven[:], picked[c][:])
+            x_codes[c] = sb("x_codes%d" % c, [P, CHUNK], U32)
+            x_planes[c] = sb("x_plane%d" % c, [P, CHUNK], U8)
             nc.vector.quantize_mx(
-                out=x_codes[:].bitcast(FP8X4), scales=x_plane[:], in_=woven[:].rearrange("p m t -> p (m t)")
+                out=x_codes[c][:].bitcast(FP8X4), scales=x_planes[c][:], in_=woven[:].rearrange("p m t -> p (m t)")
             )
+
+        def finish(c):
             cols = slice(c * CHUNK, (c + 1) * CHUNK)
-            for b in range(N_TILES // PER_BANK):
-                slot = (c * (N_TILES // PER_BANK) + b) % (PACK * HALVES)
+            for b in range(groups):
+                slot = (H_BANKS + c * groups + b) % (PACK * HALVES)
                 bank = psum.tile([P, PER_BANK, CHUNK], F32, name="y%d_%d" % (c, b), tag="bank%d" % slot)
                 for i in range(PER_BANK):
                     j = PER_BANK * b + i
@@ -214,13 +232,28 @@ def tile_list_lost_property_profiles_kernel(
                         out=bank[:, i, :],
                         lhsT=w2_codes[:, j * P : (j + 1) * P].bitcast(FP8X4),
                         lhsT_scale=w2_plane[:, j * P : (j + 1) * P],
-                        rhs=x_codes[:].bitcast(FP8X4),
-                        rhs_scale=x_plane[:],
+                        rhs=x_codes[c][:].bitcast(FP8X4),
+                        rhs_scale=x_planes[c][:],
                         start=True,
                         stop=True,
                     )
-                res = sb("res%d_%d" % (c, b), [P, PER_BANK, CHUNK], F32)
-                nc.scalar.activation(out=res[:], in_=bank[:], func=ACT.Tanh)
+                curve = sb("curve%d_%d" % (c, b), [P, PER_BANK, CHUNK], F32)
+                nc.scalar.activation(out=curve[:], in_=bank[:], func=ACT.Tanh)
                 rows = slice(PER_BANK * b, PER_BANK * (b + 1))
-                nc.vector.tensor_tensor(out=res[:], in0=res[:], in1=rel_sb[:, rows, cols], op=ALU.mult)
+                res = sb("res%d_%d" % (c, b), [P, PER_BANK, CHUNK], F32, tag=res_tags[c * groups + b])
+                nc.vector.tensor_tensor(out=res[:], in0=curve[:], in1=rel_sb[:, rows, cols], op=ALU.mult)
                 nc.sync.dma_start(out=out_rows[:, rows, cols], in_=res[:])
+
+        res_tags = ["tab0", "tab1", "tab2", "wf_raw0", "wf_raw1", "wf_raw2", "v_words0", "v_words1", "v_words2", "fresh0", "fresh1", "fresh2"]
+        pick(0)
+        pick(1)
+        quantise(0)
+        pick(2)
+        quantise(1)
+        finish(0)
+        pick(3)
+        quantise(2)
+        finish(1)
+        quantise(3)
+        finish(2)
+        finish(3)

@@ -30,7 +30,7 @@ PER_BANK = BANK // CHUNK
 LIST_COL = 16
 SCALE_ROW0 = 20
 MOVED_ROWS = 100
-H_BANKS = 3
+H_BANKS = 2
 LINE = 4
 
 
@@ -66,54 +66,56 @@ def tile_list_lost_property_profiles_kernel(
 
         for q in range(QUADS):
             nc.vector.memset(tab_sc[32 * q : 32 * q + SCALE_ROW0, :].bitcast(I32), 0)
-        nc.gpsimd.memset(wc_sc_raw[:].bitcast(I32), 0)
-        nc.gpsimd.memset(v_planes[:].bitcast(I32), 0)
+        nc.vector.memset(wc_sc_raw[:].bitcast(I32), 0)
+        nc.vector.memset(v_planes[:].bitcast(I32), 0)
 
-        def load_tab(a, queue):
+        def load_tab(a):
             words = tab_words[a].rearrange("p t i -> p (t i)").bitcast(I32)
-            queue.dma_start(out=tab[a][:].bitcast(I32), in_=words)
+            nc.sync.dma_start(out=tab[a][:].bitcast(I32), in_=words)
 
         def load_wf(a):
             rows = wf[a * P * PACK : (a + 1) * P * PACK, :]
             nc.sync.dma_start(out=wf_raw[a][:], in_=rows.rearrange("(p j) c -> p j c", j=PACK))
+
+        def load_page(t):
+            nc.sync.dma_start(out=page[t][:], in_=page_rows[t])
 
         page_rows = page0.rearrange("(g t q) c -> t g q c", t=PACK, q=RUN)
         w2_rows = w2.rearrange("(g t q) c -> t g q c", t=PACK, q=RUN)
         gain_rows = gain.rearrange("(g t q o) -> t g q o", t=PACK, q=RUN, o=1)
 
         nc.sync.dma_start(idx[:], offs)
-        load_tab(0, nc.scalar)
+        load_tab(0)
         for q in range(QUADS):
-            (nc.sync, nc.scalar)[q % 2].dma_start(
+            nc.sync.dma_start(
                 out=tab_sc[32 * q + SCALE_ROW0 : 32 * (q + 1), :].bitcast(I32),
                 in_=tab_scales[:, 4 * q : 4 * q + 4, :].bitcast(I32),
             )
-        load_tab(1, nc.sync)
-        nc.sync.dma_start(
-            out=wc_raw[:].bitcast(I32).rearrange("p (a w) -> p a w", a=PASSES),
-            in_=wc_words.bitcast(I32).rearrange("a p w -> p a w"),
-        )
+        load_tab(1)
+        load_tab(2)
         for q in range(QUADS):
             nc.sync.dma_start(
                 out=wc_sc_raw[32 * q : 32 * q + 4, :].bitcast(I32).rearrange("r (a w) -> r a w", a=PASSES),
                 in_=wc_scales[:, 4 * q : 4 * q + 4, :].bitcast(I32).rearrange("a r w -> r a w"),
             )
-        load_tab(2, nc.sync)
         load_wf(0)
+        nc.sync.dma_start(
+            out=wc_raw[:].bitcast(I32).rearrange("p (a w) -> p a w", a=PASSES),
+            in_=wc_words.bitcast(I32).rearrange("a p w -> p a w"),
+        )
         nc.sync.dma_start(idx2[:], offs2)
-        nc.sync.dma_start(out=page[0][:], in_=page_rows[0])
+        load_page(0)
         load_wf(1)
         load_wf(2)
         with nc.allow_non_contiguous_dma(reason="one gain value for each partition"):
             for t in range(PACK):
                 nc.sync.dma_start(out=gains[t][:], in_=gain_rows[t])
-        nc.sync.dma_start(out=page[1][:], in_=page_rows[1])
+        for t in range(1, PACK):
+            load_page(t)
         nc.sync.dma_start(idx3[:], offs3)
         for t in range(PACK):
             nc.sync.dma_start(out=w2_raw[:, t, :], in_=w2_rows[t])
-        nc.sync.dma_start(out=page[2][:], in_=page_rows[2])
         nc.sync.dma_start(out=rel_sb[:], in_=rel.rearrange("(j p) m -> p j m", p=P))
-        nc.sync.dma_start(out=page[3][:], in_=page_rows[3])
 
         v_words = [sb("v_words%d" % a, [P, S], U32) for a in range(PASSES)]
         v_sc = sb("v_sc", [P, S], U8)
@@ -122,7 +124,7 @@ def tile_list_lost_property_profiles_kernel(
             nc.vector.tensor_copy(v_words[a][:], tab[a][:].indirect(idx[:]))
         for a in range(PASSES):
             row0 = SCALE_ROW0 + 4 * a
-            nc.scalar.dma_start(
+            nc.gpsimd.dma_start(
                 out=v_planes[0:MOVED_ROWS, a * S : (a + 1) * S].bitcast(I32),
                 in_=v_sc[row0 : row0 + MOVED_ROWS, :].bitcast(I32),
             )
@@ -151,6 +153,15 @@ def tile_list_lost_property_profiles_kernel(
                     in_=woven[:].rearrange("p t w -> p (t w)"),
                 )
 
+        old = {}
+
+        def fetch_old(t, u):
+            old[t, u] = sb("old%d_%d" % (t, u), [P, BANK], F32, tag="old%d" % u)
+            part = idx2[:, u * BANK // LIST_COL : (u + 1) * BANK // LIST_COL]
+            nc.vector.tensor_copy(old[t, u][:], page[t][:].indirect(part))
+
+        for u in range(HALVES):
+            fetch_old(0, u)
         for t in range(PACK):
             fresh = sb("fresh%d" % t, [P, S], F32)
             banks = []
@@ -180,15 +191,16 @@ def tile_list_lost_property_profiles_kernel(
                         stop=(a == PASSES - 1),
                     )
             for u in range(HALVES):
-                part = idx2[:, u * BANK // LIST_COL : (u + 1) * BANK // LIST_COL]
-                nc.vector.tensor_copy(fresh[:, u * BANK : (u + 1) * BANK], page[t][:].indirect(part))
-            for u in range(HALVES):
                 cols = slice(u * BANK, (u + 1) * BANK)
                 nc.vector.scalar_tensor_tensor(
-                    out=fresh[:, cols], in0=banks[u][:], scalar=gains[t][:], in1=fresh[:, cols],
+                    out=fresh[:, cols], in0=banks[u][:], scalar=gains[t][:], in1=old[t, u][:],
                     op0=ALU.mult, op1=ALU.max,
                 )
+            if t + 1 < PACK:
+                fetch_old(t + 1, 0)
             nc.vector.tensor_copy(page[t][:].indirect(idx2[:]), fresh[:])
+            if t + 1 < PACK:
+                fetch_old(t + 1, 1)
 
         w2_codes = sb("w2_codes", [P, N], U32)
         w2_plane = sb("w2_plane", [P, N], U8)
@@ -203,7 +215,9 @@ def tile_list_lost_property_profiles_kernel(
 
         out_rows = out.rearrange("(j p) m -> p j m", p=P)
         groups = N_TILES // PER_BANK
-        picked_tags = ["picked0", "fresh3", "x_woven0", "curve0_%d" % (groups - 1)]
+        picked_tags = ["picked0", "fresh3", "w2_woven", "x_woven1"]
+        woven_tags = ["w2_woven", "x_woven1", "x_woven2", "x_woven3"]
+        res_tags = ["tab0", "tab1", "tab2", "wf_raw0"]
         picked, x_codes, x_planes = {}, {}, {}
 
         def pick(c):
@@ -213,7 +227,7 @@ def tile_list_lost_property_profiles_kernel(
                 nc.vector.tensor_copy(picked[c][:, t, :], page[t][:].indirect(part))
 
         def quantise(c):
-            woven = sb("x_woven%d" % c, [P, CHUNK, PACK], BF16)
+            woven = sb("x_woven%d" % c, [P, CHUNK, PACK], BF16, tag=woven_tags[c])
             weave(woven[:], picked[c][:])
             x_codes[c] = sb("x_codes%d" % c, [P, CHUNK], U32)
             x_planes[c] = sb("x_plane%d" % c, [P, CHUNK], U8)
@@ -223,6 +237,8 @@ def tile_list_lost_property_profiles_kernel(
 
         def finish(c):
             cols = slice(c * CHUNK, (c + 1) * CHUNK)
+            curve = sb("curve%d" % c, [P, N_TILES, CHUNK], F32)
+            res = sb("res%d" % c, [P, N_TILES, CHUNK], F32, tag=res_tags[c])
             for b in range(groups):
                 slot = (H_BANKS + c * groups + b) % (PACK * HALVES)
                 bank = psum.tile([P, PER_BANK, CHUNK], F32, name="y%d_%d" % (c, b), tag="bank%d" % slot)
@@ -237,23 +253,22 @@ def tile_list_lost_property_profiles_kernel(
                         start=True,
                         stop=True,
                     )
-                curve = sb("curve%d_%d" % (c, b), [P, PER_BANK, CHUNK], F32)
-                nc.scalar.activation(out=curve[:], in_=bank[:], func=ACT.Tanh)
                 rows = slice(PER_BANK * b, PER_BANK * (b + 1))
-                res = sb("res%d_%d" % (c, b), [P, PER_BANK, CHUNK], F32, tag=res_tags[c * groups + b])
-                nc.vector.tensor_tensor(out=res[:], in0=curve[:], in1=rel_sb[:, rows, cols], op=ALU.mult)
-                nc.sync.dma_start(out=out_rows[:, rows, cols], in_=res[:])
+                nc.scalar.activation(out=curve[:, rows, :], in_=bank[:], func=ACT.Tanh)
+                nc.vector.tensor_tensor(
+                    out=res[:, rows, :], in0=curve[:, rows, :], in1=rel_sb[:, rows, cols], op=ALU.mult
+                )
+                nc.sync.dma_start(out=out_rows[:, rows, cols], in_=res[:, rows, :])
 
-        res_tags = ["tab0", "tab1", "tab2", "wf_raw0", "wf_raw1", "wf_raw2", "v_words0", "v_words1", "v_words2", "fresh0", "fresh1", "fresh2"]
         pick(0)
         pick(1)
         quantise(0)
         pick(2)
         quantise(1)
-        finish(0)
         pick(3)
         quantise(2)
-        finish(1)
+        finish(0)
         quantise(3)
+        finish(1)
         finish(2)
         finish(3)

from contextlib import ExitStack

import concourse.mybir as mybir

K, T, S, H, T2, M, N = 1536, 2048, 1024, 512, 2048, 1024, 768
FLOPS = 2 * (2 * K * H * S + H * N * M)

F32 = mybir.dt.float32
BF16 = mybir.dt.bfloat16
I32 = mybir.dt.int32
U32 = mybir.dt.uint32
U16 = mybir.dt.uint16
U8 = mybir.dt.uint8
FP8X4 = mybir.dt.float8_e4m3fn_x4
FP4X4 = mybir.dt.float4_e2m1fn_x4
ALU = mybir.AluOpType
ACT = mybir.ActivationFunctionType

P = 128
PACK = 4
PASSES = K // (P * PACK)
QUADS = 4
RUN = 8
BANK = 512
HALVES = S // BANK
CHUNK = 256
CHUNKS = M // CHUNK
N_TILES = N // P
PER_BANK = BANK // CHUNK
LIST_COL = 16
SCALE_ROW0 = 20
MOVED_ROWS = 100
H_BANKS = 2
LINE = 4


def tile_list_lost_property_profiles_kernel(
    tc, tab_words, tab_scales, offs, wc_words, wc_scales, wf, gain, page0, offs2, offs3, w2, rel, out
):
    nc = tc.nc
    with ExitStack() as ctx:
        keep = ctx.enter_context(tc.tile_pool(name="keep", bufs=1))
        psum = ctx.enter_context(tc.psum_pool(name="psum", bufs=1))

        def sb(name, shape, dtype, tag=None):
            return keep.tile(shape, dtype, name=name, tag=tag or name, align_bytes=64)

        def weave(dst, src):
            nc.scalar.copy(
                out=dst.rearrange("p (c i) t -> p c t i", i=LINE), in_=src.rearrange("p t (c i) -> p c t i", i=LINE)
            )

        idx = sb("idx", [P, S // LIST_COL], U16)
        idx2 = sb("idx2", [P, S // LIST_COL], U16)
        idx3 = sb("idx3", [P, M // LIST_COL], U16)
        tab = [sb("tab%d" % a, [P, T], U32) for a in range(PASSES)]
        tab_sc = sb("tab_sc", [P, T], U8)
        v_planes = sb("v_planes", [P, PASSES * S], U8)
        wc_raw = sb("wc_raw", [P, PASSES * 2 * H], U8)
        wc_sc_raw = sb("wc_sc_raw", [P, PASSES * H], U8)
        wf_raw = [sb("wf_raw%d" % a, [P, PACK, H], F32) for a in range(PASSES)]
        page = [sb("page%d" % t, [P, T2], F32) for t in range(PACK)]
        gains = [sb("gain%d" % t, [P, 1], F32) for t in range(PACK)]
        w2_raw = sb("w2_raw", [P, PACK, N], F32)
        rel_sb = sb("rel_sb", [P, N_TILES, M], F32)

        for q in range(QUADS):
            nc.vector.memset(tab_sc[32 * q : 32 * q + SCALE_ROW0, :].bitcast(I32), 0)
        nc.vector.memset(wc_sc_raw[:].bitcast(I32), 0)
        nc.vector.memset(v_planes[:].bitcast(I32), 0)

        def load_tab(a):
            words = tab_words[a].rearrange("p t i -> p (t i)").bitcast(I32)
            nc.sync.dma_start(out=tab[a][:].bitcast(I32), in_=words)

        def load_wf(a):
            rows = wf[a * P * PACK : (a + 1) * P * PACK, :]
            nc.sync.dma_start(out=wf_raw[a][:], in_=rows.rearrange("(p j) c -> p j c", j=PACK))

        def load_page(t):
            nc.sync.dma_start(out=page[t][:], in_=page_rows[t])

        page_rows = page0.rearrange("(g t q) c -> t g q c", t=PACK, q=RUN)
        w2_rows = w2.rearrange("(g t q) c -> t g q c", t=PACK, q=RUN)
        gain_rows = gain.rearrange("(g t q o) -> t g q o", t=PACK, q=RUN, o=1)

        nc.sync.dma_start(idx[:], offs)
        load_tab(0)
        for q in range(QUADS):
            nc.sync.dma_start(
                out=tab_sc[32 * q + SCALE_ROW0 : 32 * (q + 1), :].bitcast(I32),
                in_=tab_scales[:, 4 * q : 4 * q + 4, :].bitcast(I32),
            )
        load_tab(1)
        load_tab(2)
        for q in range(QUADS):
            nc.sync.dma_start(
                out=wc_sc_raw[32 * q : 32 * q + 4, :].bitcast(I32).rearrange("r (a w) -> r a w", a=PASSES),
                in_=wc_scales[:, 4 * q : 4 * q + 4, :].bitcast(I32).rearrange("a r w -> r a w"),
            )
        load_wf(0)
        nc.sync.dma_start(
            out=wc_raw[:].bitcast(I32).rearrange("p (a w) -> p a w", a=PASSES),
            in_=wc_words.bitcast(I32).rearrange("a p w -> p a w"),
        )
        nc.sync.dma_start(idx2[:], offs2)
        load_page(0)
        load_wf(1)
        load_wf(2)
        with nc.allow_non_contiguous_dma(reason="one gain value for each partition"):
            for t in range(PACK):
                nc.sync.dma_start(out=gains[t][:], in_=gain_rows[t])
        for t in range(1, PACK):
            load_page(t)
        nc.sync.dma_start(idx3[:], offs3)
        for t in range(PACK):
            nc.sync.dma_start(out=w2_raw[:, t, :], in_=w2_rows[t])
        nc.sync.dma_start(out=rel_sb[:], in_=rel.rearrange("(j p) m -> p j m", p=P))

        v_words = [sb("v_words%d" % a, [P, S], U32) for a in range(PASSES)]
        v_sc = sb("v_sc", [P, S], U8)
        nc.vector.tensor_copy(v_sc[:], tab_sc[:].indirect(idx[:]))
        for a in range(PASSES):
            nc.vector.tensor_copy(v_words[a][:], tab[a][:].indirect(idx[:]))
        for a in range(PASSES):
            row0 = SCALE_ROW0 + 4 * a
            nc.gpsimd.dma_start(
                out=v_planes[0:MOVED_ROWS, a * S : (a + 1) * S].bitcast(I32),
                in_=v_sc[row0 : row0 + MOVED_ROWS, :].bitcast(I32),
            )

        wc_codes = sb("wc_codes", [P, PASSES * 2 * H], U8)
        wc_planes = sb("wc_planes", [P, PASSES * H], U8)
        for dealt, raw, words in ((wc_codes, wc_raw, RUN // 2), (wc_planes, wc_sc_raw, RUN // 4)):
            nc.vector.tensor_copy(
                out=dealt[:].bitcast(I32).rearrange("p (a t g w) -> p a t g w", a=PASSES, t=PACK, w=words),
                in_=raw[:].bitcast(I32).rearrange("p (a g t w) -> p a t g w", a=PASSES, t=PACK, w=words),
            )

        wf_codes = [sb("wf_codes%d" % a, [P, H], U32) for a in range(PASSES)]
        wf_planes = [sb("wf_planes%d" % a, [P, H], U8) for a in range(PASSES)]
        for a in range(PASSES):
            src = wf_raw[a][:].rearrange("p j (g t h i) -> p t g h j i", t=PACK, h=RUN // LINE, i=LINE)
            step = 1 if a == PASSES - 1 else PACK
            for t0 in range(0, PACK, step):
                woven = sb("wf_woven%d_%d" % (a, t0), [P, step, P * PACK], BF16)
                for t in range(t0, t0 + step):
                    dst = woven[:, t - t0, :].rearrange("p (g h i j) -> p g h j i", h=RUN // LINE, i=LINE, j=PACK)
                    nc.scalar.copy(out=dst, in_=src[:, t])
                cols = slice(t0 * P, (t0 + step) * P)
                nc.vector.quantize_mx(
                    out=wf_codes[a][:, cols].bitcast(FP8X4), scales=wf_planes[a][:, cols],
                    in_=woven[:].rearrange("p t w -> p (t w)"),
                )

        old = {}

        def fetch_old(t, u):
            old[t, u] = sb("old%d_%d" % (t, u), [P, BANK], F32, tag="old%d" % u)
            part = idx2[:, u * BANK // LIST_COL : (u + 1) * BANK // LIST_COL]
            nc.vector.tensor_copy(old[t, u][:], page[t][:].indirect(part))

        for u in range(HALVES):
            fetch_old(0, u)
        for t in range(PACK):
            fresh = sb("fresh%d" % t, [P, S], F32)
            banks = []
            for u in range(HALVES):
                bank = psum.tile([P, BANK], F32, name="h%d_%d" % (t, u), tag="bank%d" % ((HALVES * t + u) % H_BANKS))
                banks.append(bank)
                cols = slice(u * BANK, (u + 1) * BANK)
                for a in range(PASSES):
                    c0 = a * H + t * P
                    nc.tensor.matmul_mx(
                        out=bank[:],
                        lhsT=wc_codes[:, 2 * c0 : 2 * (c0 + P)].bitcast(FP4X4),
                        lhsT_scale=wc_planes[:, c0 : c0 + P],
                        rhs=v_words[a][:, cols].bitcast(FP8X4),
                        rhs_scale=v_planes[:, a * S + u * BANK : a * S + (u + 1) * BANK],
                        start=(a == 0),
                        stop=False,
                    )
                for a in range(PASSES):
                    nc.tensor.matmul_mx(
                        out=bank[:],
                        lhsT=wf_codes[a][:, t * P : (t + 1) * P].bitcast(FP8X4),
                        lhsT_scale=wf_planes[a][:, t * P : (t + 1) * P],
                        rhs=v_words[a][:, cols].bitcast(FP8X4),
                        rhs_scale=v_planes[:, a * S + u * BANK : a * S + (u + 1) * BANK],
                        start=False,
                        stop=(a == PASSES - 1),
                    )
            for u in range(HALVES):
                cols = slice(u * BANK, (u + 1) * BANK)
                nc.vector.scalar_tensor_tensor(
                    out=fresh[:, cols], in0=banks[u][:], scalar=gains[t][:], in1=old[t, u][:],
                    op0=ALU.mult, op1=ALU.max,
                )
            if t + 1 < PACK:
                fetch_old(t + 1, 0)
            nc.vector.tensor_copy(page[t][:].indirect(idx2[:]), fresh[:])
            if t + 1 < PACK:
                fetch_old(t + 1, 1)

        w2_codes = sb("w2_codes", [P, N], U32)
        w2_plane = sb("w2_plane", [P, N], U8)
        w2_woven = sb("w2_woven", [P, N, PACK], BF16)
        for u in range(2):
            cols = slice(u * N // 2, (u + 1) * N // 2)
            weave(w2_woven[:, cols, :], w2_raw[:, :, cols])
            nc.vector.quantize_mx(
                out=w2_codes[:, cols].bitcast(FP8X4), scales=w2_plane[:, cols],
                in_=w2_woven[:, cols, :].rearrange("p n t -> p (n t)"),
            )

        out_rows = out.rearrange("(j p) m -> p j m", p=P)
        groups = N_TILES // PER_BANK
        picked_tags = ["picked0", "fresh3", "w2_woven", "x_woven1"]
        woven_tags = ["w2_woven", "x_woven1", "x_woven2", "x_woven3"]
        res_tags = ["tab0", "tab1", "tab2", "wf_raw0"]
        picked, x_codes, x_planes = {}, {}, {}

        def pick(c):
            part = idx3[:, c * CHUNK // LIST_COL : (c + 1) * CHUNK // LIST_COL]
            picked[c] = sb("picked%d" % c, [P, PACK, CHUNK], F32, tag=picked_tags[c])
            for t in range(PACK):
                nc.vector.tensor_copy(picked[c][:, t, :], page[t][:].indirect(part))

        def quantise(c):
            woven = sb("x_woven%d" % c, [P, CHUNK, PACK], BF16, tag=woven_tags[c])
            weave(woven[:], picked[c][:])
            x_codes[c] = sb("x_codes%d" % c, [P, CHUNK], U32)
            x_planes[c] = sb("x_plane%d" % c, [P, CHUNK], U8)
            nc.vector.quantize_mx(
                out=x_codes[c][:].bitcast(FP8X4), scales=x_planes[c][:], in_=woven[:].rearrange("p m t -> p (m t)")
            )

        def finish(c):
            cols = slice(c * CHUNK, (c + 1) * CHUNK)
            curve = sb("curve%d" % c, [P, N_TILES, CHUNK], F32)
            res = sb("res%d" % c, [P, N_TILES, CHUNK], F32, tag=res_tags[c])
            for b in range(groups):
                slot = (H_BANKS + c * groups + b) % (PACK * HALVES)
                bank = psum.tile([P, PER_BANK, CHUNK], F32, name="y%d_%d" % (c, b), tag="bank%d" % slot)
                for i in range(PER_BANK):
                    j = PER_BANK * b + i
                    nc.tensor.matmul_mx(
                        out=bank[:, i, :],
                        lhsT=w2_codes[:, j * P : (j + 1) * P].bitcast(FP8X4),
                        lhsT_scale=w2_plane[:, j * P : (j + 1) * P],
                        rhs=x_codes[c][:].bitcast(FP8X4),
                        rhs_scale=x_planes[c][:],
                        start=True,
                        stop=True,
                    )
                rows = slice(PER_BANK * b, PER_BANK * (b + 1))
                nc.scalar.activation(out=curve[:, rows, :], in_=bank[:], func=ACT.Tanh)
                nc.vector.tensor_tensor(
                    out=res[:, rows, :], in0=curve[:, rows, :], in1=rel_sb[:, rows, cols], op=ALU.mult
                )
                nc.sync.dma_start(out=out_rows[:, rows, cols], in_=res[:, rows, :])

        pick(0)
        pick(1)
        quantise(0)
        pick(2)
        quantise(1)
        pick(3)
        quantise(2)
        finish(0)
        quantise(3)
        finish(1)
        finish(2)
        finish(3)
